import numpy as np
import ml_dtypes


def mxq(x, axis, fmt="e4m3"):
    dtype, down = {"e4m3": (ml_dtypes.float8_e4m3fn, 7), "e5m2": (ml_dtypes.float8_e5m2, 14)}[fmt]
    v = np.moveaxis(np.asarray(x, np.float32).astype(ml_dtypes.bfloat16).astype(np.float64), axis, -1)
    blocks = v.reshape(v.shape[:-1] + (-1, 32))
    amax = np.abs(blocks).max(-1, keepdims=True)
    byte = np.maximum(np.where(amax > 0, np.frexp(amax)[1] - 1 + 127, 0) - down, 1)
    scale = np.exp2(byte - 127.0)
    codes = (blocks / scale).astype(np.float32).astype(dtype).astype(np.float64)
    return np.moveaxis((codes * scale).reshape(v.shape), -1, axis)


WIDE = False


def mx_kscale(k):
    if not WIDE:
        return np.ones(k)
    levels = np.array([10, -10, 5, -5, 0])
    if k % 512:
        return np.exp2(np.random.permutation(np.resize(levels, k // 32))).repeat(32)
    a = np.empty((k // 512, 16))
    for p in range(k // 512):
        a[p, :8] = np.random.permutation(np.resize(levels, 8))
        for g in range(8):
            far = levels[np.abs(levels - a[p, g]) >= 10]
            a[p, g + 8] = far[np.random.randint(len(far))]
    return np.exp2(a.ravel()).repeat(32)


BF16 = ml_dtypes.bfloat16


def bf(x):
    return np.asarray(x, np.float32).astype(BF16)


def f64(x):
    return np.asarray(x).astype(np.float64)


E2M1 = np.array([0.0, 0.5, 1.0, 1.5, 2.0, 3.0, 4.0, 6.0, -0.0, -0.5, -1.0, -1.5, -2.0, -3.0, -4.0, -6.0])


def pack_weight(w, fmt):
    k, n = w.shape
    w = f64(bf(w)).reshape(k // 32, 32, n)
    amax = np.abs(w).max(1)
    if fmt == "e4m3":
        byte = np.frexp(amax)[1] - 1 + 127 - 7
    else:
        mant, ex = np.frexp(amax / 6.0)
        byte = np.where(mant > 0.5, ex, ex - 1) + 127
    byte = np.clip(np.where(amax > 0, byte, 1), 1, 254)
    scaled = (w * np.exp2(127.0 - byte)[:, None, :]).reshape(k, n).astype(np.float32)
    by_word = np.ascontiguousarray(scaled.reshape(k // 512, 128, 4, n).transpose(0, 1, 3, 2))
    if fmt == "e4m3":
        words = by_word.astype(ml_dtypes.float8_e4m3fn).view(np.uint8)
    else:
        c = by_word.astype(ml_dtypes.float4_e2m1fn).view(np.uint8) & 0xF
        words = c[..., 0::2] | (c[..., 1::2] << 4)
    return np.ascontiguousarray(words), np.ascontiguousarray(byte.astype(np.uint8).reshape(k // 512, 16, n))


def unpack_weight(words, scales, fmt):
    g, p, n, _ = words.shape
    if fmt == "e4m3":
        vals = np.ascontiguousarray(words).view(ml_dtypes.float8_e4m3fn).astype(np.float64)
    else:
        nib = np.empty((g, p, n, 4), np.uint8)
        nib[..., 0::2] = words & 0xF
        nib[..., 1::2] = words >> 4
        vals = E2M1[nib]
    vals = vals * np.repeat(np.exp2(scales.astype(np.float64) - 127.0), 8, axis=1)[..., None]
    return vals.transpose(0, 1, 3, 2).reshape(g * 512, n)
def pack4(w):
    words, scales = pack_weight(w, "e2m1")
    return words.reshape(words.shape[0], 128, -1), scales


def unpack4(words, scales):
    return unpack_weight(words.reshape(words.shape[0], 128, -1, 2), scales, "e2m1")


def planes(Y):
    n, m = Y.shape
    b = f64(bf(Y)).reshape(n // 32, 32, m)
    amax = np.abs(b).max(1)
    byte = np.clip(np.where(amax > 0, np.frexp(amax)[1] - 1 + 127 - 7, 1), 1, 254)
    codes = (b * np.exp2(127.0 - byte)[:, None, :]).reshape(n, m).astype(np.float32).astype(ml_dtypes.float8_e4m3fn).view(np.uint8)
    words = codes.reshape(n // 512, 128, 4, m).transpose(0, 1, 3, 2)
    return np.ascontiguousarray(words), np.ascontiguousarray(byte.astype(np.uint8).reshape(n // 512, 16, m))


N, D, E, G = 1024, 1024, 1024, 3


def gained_product(left, right, p_row, q_row):
    return mxq(left * p_row[None, :], 1, "e4m3") @ mxq(q_row[:, None] * right, 0, "e4m3")


def mod_relu(z, b):
    return np.sign(z) * np.maximum(np.abs(z) + b[None, :], 0.0)


def setup_inputs():
    cx = mx_kscale(E)
    c = np.stack([mx_kscale(D) for _ in range(G)])
    h = np.random.standard_normal((N, D))
    x = np.random.standard_normal((N, E)) * cx[None, :]
    a = np.random.standard_normal((D, D)) / np.sqrt(D)
    t = np.random.standard_normal((E, D)) / np.sqrt(E) / cx[:, None]
    t_words, t_scales = pack4(t)
    p = (1.0 + 0.2 * np.random.standard_normal((G, D))) * c
    q = (1.0 + 0.2 * np.random.standard_normal((G, D))) / c
    b = np.random.uniform(-0.5, -0.1, D)
    return {"h": bf(h), "x": bf(x), "a": bf(a), "t_words": t_words, "t_scales": t_scales, "p": bf(p), "q": bf(q), "b": bf(b)}


def core(h, x, a, t_words, t_scales, p, q, b):
    h, x, a, p, q, b = f64(h), f64(x), f64(a), f64(p), f64(q), f64(b)
    s = a - a.T
    k1 = gained_product(h, s, p[0], q[0])
    s2 = gained_product(s, s, p[1], q[1])
    r = s / 2.0 + s2 / 6.0
    k23 = gained_product(k1, r, p[2], q[2])
    u = mxq(x, 1, "e4m3") @ unpack4(t_words, t_scales)
    z = h + k1 + k23 + u
    return mod_relu(z, b)


def reference(h, x, a, t_words, t_scales, p, q, b):
    R_out = core(h, x, a, t_words, t_scales, p, q, b)
    words, scales = planes(R_out)
    return R_out, words, scales

@@ -1,0 +1,391 @@
+from contextlib import ExitStack
+
+import concourse.mybir as mybir
+from concourse.masks import make_identity
+
+F32 = mybir.dt.float32
+BF16 = mybir.dt.bfloat16
+I32 = mybir.dt.int32
+U32 = mybir.dt.uint32
+U8 = mybir.dt.uint8
+FP8X4 = mybir.dt.float8_e4m3fn_x4
+FP4X4 = mybir.dt.float4_e2m1fn_x4
+ALU = mybir.AluOpType
+ACT = mybir.ActivationFunctionType
+
+P = 128
+N = 1024
+HALF = 512
+ST_BUFS = 7
+FLOPS = 4 * 2 * N * N * N
+
+P0, P1, P2, Q0, Q1, Q2 = range(6)
+NEG_P1, Q2_HALF, Q2_SIXTH = range(3)
+
+
+def tile_skewexptaylorrecurrentstep_x2_kernel(tc, h, x, a, t_words, t_scales, p, q, b, out_0, out_1, out_2):
+    nc = tc.nc
+    with ExitStack() as ctx:
+        keep = ctx.enter_context(tc.tile_pool(name="keep", bufs=1))
+        psum = ctx.enter_context(tc.psum_pool(name="psum", bufs=8))
+
+        def bank():
+            bank_t = psum.tile([P, HALF], F32, name="bank")
+            return bank_t
+
+        def operand(nm):
+            codes = keep.tile([P, 2, N], U32, align_bytes=64, name=nm + "_codes")
+            scales = keep.tile([P, 2, N], U8, align_bytes=64, name=nm + "_scales")
+            return codes, scales
+
+        def quantize(op, g, c0, il):
+            codes, scales = op
+            nc.vector.quantize_mx(
+                out=codes[:, g, c0 : c0 + HALF].bitcast(FP8X4),
+                scales=scales[:, g, c0 : c0 + HALF],
+                in_=il[:].rearrange("p c t -> p (c t)"),
+            )
+
+        def interleave(il, st, eng="v"):
+            (nc.vector.tensor_copy if eng == "v" else nc.scalar.copy)(
+                out=il[:].rearrange("p (c i) t -> p c t i", i=4),
+                in_=st[:].rearrange("p t (c i) -> p c t i", i=4),
+            )
+
+        op_h, op_x, op_k1, op_r = operand("h"), operand("x"), operand("k1"), operand("r")
+        op_p1, op_q1, op_q0, op_q0p = operand("p1"), operand("q1"), operand("q0"), operand("q0p")
+        g_sb = keep.tile([P, 8, N], F32, name="g_sb")
+        h_sb = keep.tile([P, 8, N], BF16, align_bytes=64, name="h_sb")
+        t_sb = keep.tile([P, 2, 2 * N], U8, align_bytes=64, name="t_sb")
+        t_sc = keep.tile([P, 2, N], U8, align_bytes=64, name="t_sc")
+        b_sb = keep.tile([P, N], BF16, name="b_sb")
+        gn = keep.tile([P, 8, 8], F32, name="gn")
+        dv = keep.tile([P, 3, 8], F32, name="dv")
+        p0b = keep.tile([P, 8], BF16, name="p0b")
+        ident = keep.tile([P, P], BF16, name="ident")
+        nident = keep.tile([P, P], BF16, name="nident")
+        ident_f = keep.tile([P, P], F32, name="ident_f")
+
+        def scaled(eng, out, in_, sc):
+            if eng == "s":
+                nc.scalar.activation(out=out, in_=in_, func=ACT.Copy, scale=sc)
+            else:
+                nc.vector.tensor_scalar(out=out, in0=in_, scalar1=sc, scalar2=None, op0=ALU.mult)
+
+        def product(out, left, m0, right, n0, start=True, stop=True):
+            for g in range(2):
+                nc.tensor.matmul_mx(
+                    out=out,
+                    lhsT=left[0][:, g, m0 : m0 + P].bitcast(FP8X4),
+                    lhsT_scale=left[1][:, g, m0 : m0 + P],
+                    rhs=right[0][:, g, n0 : n0 + HALF].bitcast(FP8X4),
+                    rhs_scale=right[1][:, g, n0 : n0 + HALF],
+                    start=start and g == 0,
+                    stop=stop and g == 1,
+                )
+
+        def product_t(out, m0, n0):
+            for g in range(2):
+                nc.tensor.matmul_mx(
+                    out=out,
+                    lhsT=op_x[0][:, g, m0 : m0 + P].bitcast(FP8X4),
+                    lhsT_scale=op_x[1][:, g, m0 : m0 + P],
+                    rhs=t_sb[:, g, 2 * n0 : 2 * n0 + 2 * HALF].bitcast(FP4X4),
+                    rhs_scale=t_sc[:, g, n0 : n0 + HALF],
+                    start=g == 0,
+                    stop=False,
+                )
+
+        stage = ctx.enter_context(tc.tile_pool(name="stage", bufs=2))
+
+        with ExitStack() as st1:
+            early = st1.enter_context(tc.tile_pool(name="early", bufs=1))
+
+            pq = early.tile([P, N], BF16, name="pq")
+            nc.vector.memset(pq[:].bitcast(U32), 0)
+            nc.scalar.dma_start(out=pq[0:3, :], in_=p)
+            nc.scalar.dma_start(out=pq[3:6, :], in_=q)
+            make_identity(nc, ident[:])
+            make_identity(nc, ident_f[:])
+            nc.vector.tensor_scalar(out=nident[:], in0=ident[:], scalar1=-1.0, scalar2=None, op0=ALU.mult)
+            nc.gpsimd.memset(t_sc[:].rearrange("p g n -> p (g n)").bitcast(I32), 0)
+            nc.gpsimd.memset(op_q0[1][:].rearrange("p g n -> p (g n)").bitcast(I32), 0)
+
+            quads = [(0, 0), (0, 1), (1, 0), (1, 1)]
+            a_nat, a_perm = {}, {}
+            for i, (ch, g) in enumerate(quads):
+                an = early.tile([P, 4, HALF], BF16, name="an%d%d" % (ch, g))
+                ap = early.tile([P, 4, HALF], BF16, name="ap%d%d" % (ch, g))
+                nc.sync.dma_start(
+                    out=an[:],
+                    in_=a[HALF * ch : HALF * ch + HALF, HALF * g : HALF * g + HALF].rearrange("(k c) e -> c k e", c=P),
+                )
+                src = a[HALF * g : HALF * g + HALF, HALF * ch : HALF * ch + HALF].rearrange("(c t) e -> c t e", t=4)
+                for t0, t1 in ((0, 1), (1, 2), (2, 4)) if i == 0 else ((0, 4),):
+                    nc.sync.dma_start(out=ap[:, t0:t1, :], in_=src[:, t0:t1, :])
+                a_nat[ch, g], a_perm[ch, g] = an, ap
+            for g in range(2):
+                nc.sync.dma_start(out=h_sb[:, 4 * g : 4 * g + 4, :], in_=h[HALF * g : HALF * g + HALF, :].rearrange("(c t) e -> c t e", t=4))
+            x_sb = early.tile([P, 8, N], BF16, align_bytes=64, name="x_sb")
+            for g in range(2):
+                nc.sync.dma_start(out=x_sb[:, 4 * g : 4 * g + 4, :], in_=x[HALF * g : HALF * g + HALF, :].rearrange("(c t) e -> c t e", t=4))
+            for g in range(2):
+                nc.sync.dma_start(out=t_sb[:, g, :].bitcast(I32), in_=t_words[g].bitcast(I32))
+            for qd in range(4):
+                nc.sync.dma_start(
+                    out=t_sc[32 * qd : 32 * qd + 4, :, :].bitcast(I32),
+                    in_=t_scales[:, 4 * qd : 4 * qd + 4, :].rearrange("g r n -> r g n").bitcast(I32),
+                )
+            nc.sync.dma_start(out=b_sb[:], in_=b.partition_broadcast(P))
+
+            gps = psum.tile([P, 8, P], BF16, name="bank")
+            for gt in range(8):
+                g, t = gt // 4, gt % 4
+                nc.tensor.transpose(gps[:, gt, :], pq[:, HALF * g + t : HALF * (g + 1) : 4], ident[:])
+            nc.vector.tensor_copy(out=gn[:], in_=gps[:, :, 0:8])
+            nc.vector.tensor_scalar(out=dv[:, NEG_P1, :], in0=gn[:, :, P1], scalar1=-1.0, scalar2=None, op0=ALU.mult)
+            nc.vector.tensor_scalar(out=dv[:, Q2_HALF, :], in0=gn[:, :, Q2], scalar1=0.5, scalar2=None, op0=ALU.mult)
+            nc.vector.tensor_scalar(out=dv[:, Q2_SIXTH, :], in0=gn[:, :, Q2], scalar1=1.0 / 6.0, scalar2=None, op0=ALU.mult)
+            nc.vector.tensor_copy(out=p0b[:], in_=gn[:, :, P0])
+
+            def skew_quad(ch, g, who):
+                sq0 = stage.tile([P, 4, HALF], BF16, name="st", bufs=ST_BUFS)
+                sq1 = stage.tile([P, 4, HALF], BF16, name="st", bufs=ST_BUFS)
+                sp1 = stage.tile([P, 4, HALF], BF16, name="st", bufs=ST_BUFS)
+                for t in range(4):
+                    gt = 4 * g + t
+                    s = bank()
+                    nc.tensor.matmul(s[:], lhsT=ident[:], rhs=a_perm[ch, g][:, t, :], start=True, stop=False)
+                    for k in range(4):
+                        nc.tensor.matmul(
+                            s[:, P * k : P * k + P],
+                            lhsT=a_nat[ch, g][:, k, t:HALF:4],
+                            rhs=nident[:],
+                            start=False,
+                            stop=(k == 3),
+                        )
+                    w = who[t]
+                    scaled(w[0], sq0[:, t, :], s[:], gn[:, gt, Q0 : Q0 + 1])
+                    scaled(w[1], sp1[:, t, :].rearrange("p (q m) -> p q m", q=4), s[:].rearrange("p (m q) -> p q m", q=4), dv[:, NEG_P1, gt : gt + 1])
+                    scaled(w[2], sq1[:, t, :], s[:], gn[:, gt, Q1 : Q1 + 1])
+                    scaled(w[3], g_sb[:, gt, HALF * ch : HALF * ch + HALF], s[:], dv[:, Q2_HALF, gt : gt + 1])
+                return sq0, sp1, sq1
+
+            def il_tile():
+                il = stage.tile([P, HALF, 4], BF16, align_bytes=64, name="il", bufs=4)
+                return il
+
+            def skew_quantize(i, sts):
+                ch, g = quads[i]
+                pend = None
+                for st, op in zip(sts, (op_q0, op_p1, op_q1)):
+                    il = il_tile()
+                    interleave(il, st)
+                    if pend is not None:
+                        quantize(pend[0], g, HALF * ch, pend[1])
+                    pend = (op, il)
+                return lambda: quantize(pend[0], g, HALF * ch, pend[1])
+
+            def h_part(n, g):
+                il = il_tile()
+                words = h_sb[:].bitcast(F32)
+                for r in range(2):
+                    ht = psum.tile([P, 2, P, 2], F32, name="bank")
+                    for k in range(2):
+                        for u in range(2):
+                            nc.tensor.transpose(ht[:, k, :, u], words[:, 4 * n + 2 * r + k, 256 * g + u : 256 * (g + 1) : 2], ident_f[:])
+                    nc.vector.tensor_tensor(
+                        out=il[:, 256 * r : 256 * r + 256, :],
+                        in0=ht[:].rearrange("p k r u -> p (k r u)").bitcast(BF16).rearrange("p (c t) -> p c t", t=4),
+                        in1=p0b[:, 4 * g : 4 * g + 4].unsqueeze(1).to_broadcast([P, 256, 4]),
+                        op=ALU.mult,
+                    )
+                return lambda: quantize(op_h, g, HALF * n, il)
+
+            def x_part(n, g):
+                il = il_tile()
+                words = x_sb[:].bitcast(F32)
+                for r in range(2):
+                    xt = psum.tile([P, 2, 2, P], F32, name="bank")
+                    for k in range(2):
+                        for u in range(2):
+                            nc.tensor.transpose(xt[:, k, u, :], words[:, 4 * n + 2 * r + k, 256 * g + u : 256 * (g + 1) : 2], ident_f[:])
+                    nc.scalar.copy(
+                        out=il[:, 256 * r : 256 * r + 256, :].rearrange("p c t -> p (c t)").bitcast(F32).rearrange("p (k r u) -> p k r u", k=2, u=2),
+                        in_=xt[:].rearrange("p k u r -> p k r u"),
+                    )
+                return lambda: quantize(op_x, g, HALF * n, il)
+
+            def permute_q0(j):
+                for g in range(2):
+                    nc.vector.tensor_copy(
+                        out=op_q0p[0][:, g, HALF * j : HALF * j + HALF].bitcast(I32).rearrange("p (q m) -> p q m", q=4),
+                        in_=op_q0[0][:, g, HALF * j : HALF * j + HALF].bitcast(I32).rearrange("p (m q) -> p q m", q=4),
+                    )
+                    nc.vector.tensor_copy(
+                        out=op_q0p[1][:, g, HALF * j : HALF * j + HALF].rearrange("p (q m) -> p q m", q=4),
+                        in_=op_q0[1][:, g, HALF * j : HALF * j + HALF].rearrange("p (m q) -> p q m", q=4),
+                    )
+
+            def k1_banks(j, n):
+                st = stage.tile([P, 4, HALF], BF16, name="st", bufs=ST_BUFS)
+                for t in range(4):
+                    kb = bank()
+                    product(kb[:], op_q0p, HALF * j + P * t, op_h, HALF * n)
+                    scaled("s", st[:, t, :], kb[:], gn[:, 4 * j + t, P2 : P2 + 1])
+                return st
+
+            def k1_quantize(j, n, st, eng="v"):
+                il = il_tile()
+                interleave(il, st, eng)
+                return lambda: quantize(op_k1, j, HALF * n, il)
+
+            st0 = skew_quad(*quads[0], who=["svsv"] * 4)
+            st1_ = skew_quad(*quads[1], who=["ssss"] * 4)
+            q = skew_quantize(0, st0)
+            q2 = h_part(0, 0)
+            q()
+            q = h_part(0, 1)
+            q2()
+            st2 = skew_quad(*quads[2], who=["ssss"] * 4)
+            q2 = skew_quantize(1, st1_)
+            q()
+            q = h_part(1, 0)
+            q2()
+            q2 = h_part(1, 1)
+            q()
+            permute_q0(0)
+            q2()
+            st3 = skew_quad(*quads[3], who=["ssss"] * 4)
+            q = skew_quantize(2, st2)
+            k00 = k1_banks(0, 0)
+            q()
+            q = skew_quantize(3, st3)
+            k01 = k1_banks(0, 1)
+            q2 = k1_quantize(0, 0, k00, "s")
+            q()
+            permute_q0(1)
+            q2()
+            xq = x_part(0, 0)
+            q = k1_quantize(0, 1, k01)
+            xq()
+            xq = x_part(0, 1)
+            q()
+            k10 = k1_banks(1, 0)
+            xq()
+            xq = x_part(1, 0)
+            q = k1_quantize(1, 0, k10)
+            xq()
+            xq = x_part(1, 1)
+            q()
+            k11 = k1_banks(1, 1)
+            xq()
+            q = k1_quantize(1, 1, k11)
+
+        late = ctx.enter_context(tc.tile_pool(name="late", bufs=2))
+
+        def r_banks(dh, j):
+            tt = late.tile([P, 4, HALF], F32, name="tt")
+            for t in range(4):
+                sb = bank()
+                product(sb[:], op_p1, HALF * j + P * t, op_q1, HALF * dh)
+                scaled("s", tt[:, t, :], sb[:], dv[:, Q2_SIXTH, 4 * j + t : 4 * j + t + 1])
+            return tt
+
+        def r_quantize(dh, j, tt):
+            il = il_tile()
+            nc.vector.tensor_tensor(
+                out=il[:].rearrange("p (c i) t -> p c t i", i=4),
+                in0=tt[:].rearrange("p t (c i) -> p c t i", i=4),
+                in1=g_sb[:, 4 * j : 4 * j + 4, HALF * dh : HALF * dh + HALF].rearrange("p t (c i) -> p c t i", i=4),
+                op=ALU.add,
+            )
+            return lambda: quantize(op_r, j, HALF * dh, il)
+
+        pend = q
+        for dh in range(2):
+            for j in range(2):
+                tt = r_banks(dh, j)
+                nxt = r_quantize(dh, j, tt)
+                pend()
+                pend = nxt
+        pend()
+
+        units = [(dh, g, t) for dh in range(2) for g in range(2) for t in range(4)]
+        state = {}
+
+        def z_bank(dh, g, t):
+            zb = bank()
+            m0, d0 = HALF * g + P * t, HALF * dh
+            product_t(zb[:], m0, d0)
+            product(zb[:], op_h, m0, op_q0, d0, start=False, stop=False)
+            product(zb[:], op_k1, m0, op_r, d0, start=False, stop=True)
+            return zb
+
+        def add_h(i):
+            dh, g, t = units[i]
+            zb = z_bank(dh, g, t)
+            z = late.tile([P, HALF], F32, name="z", bufs=3)
+            nc.vector.tensor_tensor(out=z[:], in0=zb[:], in1=h_sb[:, 4 * g + t, HALF * dh : HALF * dh + HALF], op=ALU.add)
+            az = late.tile([P, HALF], F32, name="az", bufs=4)
+            nc.scalar.activation(out=az[:], in_=z[:], func=ACT.Abs)
+            sg = late.tile([P, HALF], BF16, name="sg", bufs=4)
+            nc.scalar.activation(out=sg[:], in_=z[:], func=ACT.Sign)
+            state[i] = az, sg
+
+        def add_b(i):
+            dh, g, t = units[i]
+            az, sg = state[i]
+            nc.vector.tensor_tensor(out=az[:], in0=az[:], in1=b_sb[:, HALF * dh : HALF * dh + HALF], op=ALU.add)
+
+        def signed(i):
+            dh, g, t = units[i]
+            az, sg = state[i]
+            if t == 0:
+                o = late.tile([P, 4, HALF], F32, name="o")
+                state["o", dh, g] = o
+            o = state["o", dh, g]
+            nc.vector.scalar_tensor_tensor(out=o[:, t, :], in0=az[:], scalar=0.0, in1=sg[:], op0=ALU.max, op1=ALU.mult)
+            nc.sync.dma_start(
+                out=out_0[HALF * g : HALF * g + HALF, HALF * dh : HALF * dh + HALF].rearrange("(c t) e -> c t e", t=4)[:, t, :], in_=o[:, t, :]
+            )
+
+        def plane_chunk(dh, g, k):
+            o = state["o", dh, g]
+            if k == 0:
+                il = il_tile()
+                state["il"] = il
+            il = state["il"]
+            nc.scalar.copy(
+                out=il[:, P * k : P * k + P, :].rearrange("p (c i) t -> p c t i", i=4),
+                in_=o[:, :, P * k : P * k + P].rearrange("p t (c i) -> p c t i", i=4),
+            )
+            if k == 3:
+                oc = late.tile([P, HALF], U32, align_bytes=64, name="oc")
+                os_t = late.tile([P, HALF], U8, align_bytes=64, name="os_t")
+                nc.vector.quantize_mx(out=oc[:].bitcast(FP8X4), scales=os_t[:], in_=il[:].rearrange("p c t -> p (c t)"))
+                d0 = HALF * dh
+                nc.sync.dma_start(
+                    out=out_1[g, :, d0 : d0 + HALF, :].rearrange("p m t -> p (m t)").bitcast(I32), in_=oc[:].bitcast(I32)
+                )
+                for qd in range(4):
+                    nc.sync.dma_start(
+                        out=out_2[g, 4 * qd : 4 * qd + 4, d0 : d0 + HALF].bitcast(I32),
+                        in_=os_t[32 * qd : 32 * qd + 4, :].bitcast(I32),
+                    )
+
+        chunks = []
+        for i in range(18):
+            if i >= 2:
+                add_b(i - 2)
+            if i < 16:
+                add_h(i)
+            if chunks:
+                plane_chunk(*chunks.pop(0))
+            if i >= 2:
+                signed(i - 2)
+                dh, g, t = units[i - 2]
+                if t == 3:
+                    chunks += [(dh, g, k) for k in range(4)]
+        for c in chunks:
+            plane_chunk(*c)

@@ -16,7 +16,14 @@ ACT = mybir.ActivationFunctionType
 P = 128
 N = 1024
 HALF = 512
-ST_BUFS = 7
+ST_BUFS = 6
+SEQ1 = [
+    ("quad", 0, 0, "svsv"), ("quad", 1, 0, "ssss"), ("sq", 0, 0, "vvv"), ("h", 0, 0), ("h", 0, 1),
+    ("quad", 2, 0, "ssss"), ("sq", 1, 0, "vvv"), ("h", 1, 0), ("h", 1, 1), ("perm", 0, 0),
+    ("quad", 3, 0, "ssss"), ("sq", 2, 0, "vvv"), ("rb", 0, 0), ("kb", 0, 0), ("sq", 3, 0, "vvv"), ("rq", 0, 0), ("kb", 0, 1), ("kq", 0, 0, "s"), ("perm", 1, 0),
+    ("rb", 0, 1), ("kq", 0, 1, "v"), ("rq", 0, 1), ("x", 0, 0), ("x", 0, 1), ("kb", 1, 0), ("kq", 1, 0, "v"), ("x", 1, 0), ("kb", 1, 1), ("x", 1, 1), ("kq", 1, 1, "v"),
+    ("rb", 1, 0), ("rq", 1, 0), ("rb", 1, 1), ("rq", 1, 1),
+]
 FLOPS = 4 * 2 * N * N * N
 
 P0, P1, P2, Q0, Q1, Q2 = range(6)
@@ -102,33 +109,31 @@ def tile_skewexptaylorrecurrentstep_x2_kernel(tc, h, x, a, t_words, t_scales, p,
             early = st1.enter_context(tc.tile_pool(name="early", bufs=1))
 
             pq = early.tile([P, N], BF16, name="pq")
-            nc.vector.memset(pq[:].bitcast(U32), 0)
-            nc.scalar.dma_start(out=pq[0:3, :], in_=p)
-            nc.scalar.dma_start(out=pq[3:6, :], in_=q)
+            nc.gpsimd.memset(pq[:].bitcast(U32), 0)
             make_identity(nc, ident[:])
-            make_identity(nc, ident_f[:])
             nc.vector.tensor_scalar(out=nident[:], in0=ident[:], scalar1=-1.0, scalar2=None, op0=ALU.mult)
+            make_identity(nc, ident_f[:])
             nc.gpsimd.memset(t_sc[:].rearrange("p g n -> p (g n)").bitcast(I32), 0)
             nc.gpsimd.memset(op_q0[1][:].rearrange("p g n -> p (g n)").bitcast(I32), 0)
 
             quads = [(0, 0), (0, 1), (1, 0), (1, 1)]
             a_nat, a_perm = {}, {}
             for i, (ch, g) in enumerate(quads):
-                an = early.tile([P, 4, HALF], BF16, name="an%d%d" % (ch, g))
-                ap = early.tile([P, 4, HALF], BF16, name="ap%d%d" % (ch, g))
+                an = early.tile([P, 4, HALF], BF16, align_bytes=64, name="raw", bufs=8)
+                ap = early.tile([P, 4, HALF], BF16, align_bytes=64, name="raw", bufs=8)
                 nc.sync.dma_start(
                     out=an[:],
                     in_=a[HALF * ch : HALF * ch + HALF, HALF * g : HALF * g + HALF].rearrange("(k c) e -> c k e", c=P),
                 )
+                if i == 0:
+                    nc.sync.dma_start(out=pq[0:3, :], in_=p)
+                    nc.sync.dma_start(out=pq[3:6, :], in_=q)
                 src = a[HALF * g : HALF * g + HALF, HALF * ch : HALF * ch + HALF].rearrange("(c t) e -> c t e", t=4)
                 for t0, t1 in ((0, 1), (1, 2), (2, 4)) if i == 0 else ((0, 4),):
                     nc.sync.dma_start(out=ap[:, t0:t1, :], in_=src[:, t0:t1, :])
                 a_nat[ch, g], a_perm[ch, g] = an, ap
             for g in range(2):
                 nc.sync.dma_start(out=h_sb[:, 4 * g : 4 * g + 4, :], in_=h[HALF * g : HALF * g + HALF, :].rearrange("(c t) e -> c t e", t=4))
-            x_sb = early.tile([P, 8, N], BF16, align_bytes=64, name="x_sb")
-            for g in range(2):
-                nc.sync.dma_start(out=x_sb[:, 4 * g : 4 * g + 4, :], in_=x[HALF * g : HALF * g + HALF, :].rearrange("(c t) e -> c t e", t=4))
             for g in range(2):
                 nc.sync.dma_start(out=t_sb[:, g, :].bitcast(I32), in_=t_words[g].bitcast(I32))
             for qd in range(4):
@@ -137,6 +142,13 @@ def tile_skewexptaylorrecurrentstep_x2_kernel(tc, h, x, a, t_words, t_scales, p,
                     in_=t_scales[:, 4 * qd : 4 * qd + 4, :].rearrange("g r n -> r g n").bitcast(I32),
                 )
             nc.sync.dma_start(out=b_sb[:], in_=b.partition_broadcast(P))
+            x_raw = []
+            for i in range(4):
+                xr = early.tile([P, 2, N], BF16, align_bytes=64, name="raw", bufs=8)
+                nc.sync.dma_start(
+                    out=xr[:], in_=x[HALF * (i // 2) : HALF * (i // 2) + HALF, :].rearrange("(c t) e -> c t e", t=4)[:, 2 * (i % 2) : 2 * (i % 2) + 2, :]
+                )
+                x_raw.append(xr)
 
             gps = psum.tile([P, 8, P], BF16, name="bank")
             for gt in range(8):
@@ -175,16 +187,12 @@ def tile_skewexptaylorrecurrentstep_x2_kernel(tc, h, x, a, t_words, t_scales, p,
                 il = stage.tile([P, HALF, 4], BF16, align_bytes=64, name="il", bufs=4)
                 return il
 
-            def skew_quantize(i, sts):
+            def skew_quantize(i, sts, eng="vvv"):
                 ch, g = quads[i]
-                pend = None
-                for st, op in zip(sts, (op_q0, op_p1, op_q1)):
+                for st, op, e in zip(sts, (op_q0, op_p1, op_q1), eng):
                     il = il_tile()
-                    interleave(il, st)
-                    if pend is not None:
-                        quantize(pend[0], g, HALF * ch, pend[1])
-                    pend = (op, il)
-                return lambda: quantize(pend[0], g, HALF * ch, pend[1])
+                    interleave(il, st, e)
+                    quantize(op, g, HALF * ch, il)
 
             def h_part(n, g):
                 il = il_tile()
@@ -200,21 +208,20 @@ def tile_skewexptaylorrecurrentstep_x2_kernel(tc, h, x, a, t_words, t_scales, p,
                         in1=p0b[:, 4 * g : 4 * g + 4].unsqueeze(1).to_broadcast([P, 256, 4]),
                         op=ALU.mult,
                     )
-                return lambda: quantize(op_h, g, HALF * n, il)
+                quantize(op_h, g, HALF * n, il)
 
             def x_part(n, g):
                 il = il_tile()
-                words = x_sb[:].bitcast(F32)
                 for r in range(2):
                     xt = psum.tile([P, 2, 2, P], F32, name="bank")
                     for k in range(2):
                         for u in range(2):
-                            nc.tensor.transpose(xt[:, k, u, :], words[:, 4 * n + 2 * r + k, 256 * g + u : 256 * (g + 1) : 2], ident_f[:])
+                            nc.tensor.transpose(xt[:, k, u, :], x_raw[2 * n + r][:].bitcast(F32)[:, k, 256 * g + u : 256 * (g + 1) : 2], ident_f[:])
                     nc.scalar.copy(
                         out=il[:, 256 * r : 256 * r + 256, :].rearrange("p c t -> p (c t)").bitcast(F32).rearrange("p (k r u) -> p k r u", k=2, u=2),
                         in_=xt[:].rearrange("p k u r -> p k r u"),
                     )
-                return lambda: quantize(op_x, g, HALF * n, il)
+                quantize(op_x, g, HALF * n, il)
 
             def permute_q0(j):
                 for g in range(2):
@@ -238,80 +245,53 @@ def tile_skewexptaylorrecurrentstep_x2_kernel(tc, h, x, a, t_words, t_scales, p,
             def k1_quantize(j, n, st, eng="v"):
                 il = il_tile()
                 interleave(il, st, eng)
-                return lambda: quantize(op_k1, j, HALF * n, il)
+                quantize(op_k1, j, HALF * n, il)
 
-            st0 = skew_quad(*quads[0], who=["svsv"] * 4)
-            st1_ = skew_quad(*quads[1], who=["ssss"] * 4)
-            q = skew_quantize(0, st0)
-            q2 = h_part(0, 0)
-            q()
-            q = h_part(0, 1)
-            q2()
-            st2 = skew_quad(*quads[2], who=["ssss"] * 4)
-            q2 = skew_quantize(1, st1_)
-            q()
-            q = h_part(1, 0)
-            q2()
-            q2 = h_part(1, 1)
-            q()
-            permute_q0(0)
-            q2()
-            st3 = skew_quad(*quads[3], who=["ssss"] * 4)
-            q = skew_quantize(2, st2)
-            k00 = k1_banks(0, 0)
-            q()
-            q = skew_quantize(3, st3)
-            k01 = k1_banks(0, 1)
-            q2 = k1_quantize(0, 0, k00, "s")
-            q()
-            permute_q0(1)
-            q2()
-            xq = x_part(0, 0)
-            q = k1_quantize(0, 1, k01)
-            xq()
-            xq = x_part(0, 1)
-            q()
-            k10 = k1_banks(1, 0)
-            xq()
-            xq = x_part(1, 0)
-            q = k1_quantize(1, 0, k10)
-            xq()
-            xq = x_part(1, 1)
-            q()
-            k11 = k1_banks(1, 1)
-            xq()
-            q = k1_quantize(1, 1, k11)
+
+            def r_banks(dh, j):
+                tt = stage.tile([P, 4, HALF], F32, name="tt")
+                for t in range(4):
+                    sb = bank()
+                    product(sb[:], op_p1, HALF * j + P * t, op_q1, HALF * dh)
+                    scaled("s", tt[:, t, :], sb[:], dv[:, Q2_SIXTH, 4 * j + t : 4 * j + t + 1])
+                return tt
+
+            def r_quantize(dh, j, tt):
+                il = il_tile()
+                nc.vector.tensor_tensor(
+                    out=il[:].rearrange("p (c i) t -> p c t i", i=4),
+                    in0=tt[:].rearrange("p t (c i) -> p c t i", i=4),
+                    in1=g_sb[:, 4 * j : 4 * j + 4, HALF * dh : HALF * dh + HALF].rearrange("p t (c i) -> p c t i", i=4),
+                    op=ALU.add,
+                )
+                quantize(op_r, j, HALF * dh, il)
+
+            held = {}
+            for step in SEQ1:
+                kind, u, v = step[0], step[1], step[2]
+                if kind == "quad":
+                    held["st", u] = skew_quad(*quads[u], who=[step[3]] * 4)
+                elif kind == "sq":
+                    skew_quantize(u, held["st", u], step[3])
+                elif kind == "h":
+                    h_part(u, v)
+                elif kind == "x":
+                    x_part(u, v)
+                elif kind == "perm":
+                    permute_q0(u)
+                elif kind == "kb":
+                    held["k", u, v] = k1_banks(u, v)
+                elif kind == "kq":
+                    k1_quantize(u, v, held["k", u, v], step[3])
+                elif kind == "rb":
+                    held["r", u, v] = r_banks(u, v)
+                elif kind == "rq":
+                    r_quantize(u, v, held["r", u, v])
 
         late = ctx.enter_context(tc.tile_pool(name="late", bufs=2))
-
-        def r_banks(dh, j):
-            tt = late.tile([P, 4, HALF], F32, name="tt")
-            for t in range(4):
-                sb = bank()
-                product(sb[:], op_p1, HALF * j + P * t, op_q1, HALF * dh)
-                scaled("s", tt[:, t, :], sb[:], dv[:, Q2_SIXTH, 4 * j + t : 4 * j + t + 1])
-            return tt
-
-        def r_quantize(dh, j, tt):
-            il = il_tile()
-            nc.vector.tensor_tensor(
-                out=il[:].rearrange("p (c i) t -> p c t i", i=4),
-                in0=tt[:].rearrange("p t (c i) -> p c t i", i=4),
-                in1=g_sb[:, 4 * j : 4 * j + 4, HALF * dh : HALF * dh + HALF].rearrange("p t (c i) -> p c t i", i=4),
-                op=ALU.add,
-            )
-            return lambda: quantize(op_r, j, HALF * dh, il)
-
-        pend = q
-        for dh in range(2):
-            for j in range(2):
-                tt = r_banks(dh, j)
-                nxt = r_quantize(dh, j, tt)
-                pend()
-                pend = nxt
-        pend()
-
-        units = [(dh, g, t) for dh in range(2) for g in range(2) for t in range(4)]
+        QUART = HALF // 2
+        units = [(dh, g, t, 0, HALF) for dh in range(2) for g in range(2) for t in range(4)]
+        units = units[:12] + [(1, 1, t, QUART * c, QUART) for c in range(2) for t in range(4)]
         state = {}
 
         def z_bank(dh, g, t):
@@ -323,69 +303,74 @@ def tile_skewexptaylorrecurrentstep_x2_kernel(tc, h, x, a, t_words, t_scales, p,
             return zb
 
         def add_h(i):
-            dh, g, t = units[i]
-            zb = z_bank(dh, g, t)
+            dh, g, t, c0, w = units[i]
+            if c0 == 0:
+                state["z", dh, g, t] = z_bank(dh, g, t)
+            zb = state["z", dh, g, t]
+            d0 = HALF * dh + c0
             z = late.tile([P, HALF], F32, name="z", bufs=3)
-            nc.vector.tensor_tensor(out=z[:], in0=zb[:], in1=h_sb[:, 4 * g + t, HALF * dh : HALF * dh + HALF], op=ALU.add)
+            nc.vector.tensor_tensor(out=z[:, :w], in0=zb[:, c0 : c0 + w], in1=h_sb[:, 4 * g + t, d0 : d0 + w], op=ALU.add)
             az = late.tile([P, HALF], F32, name="az", bufs=4)
-            nc.scalar.activation(out=az[:], in_=z[:], func=ACT.Abs)
+            nc.scalar.activation(out=az[:, :w], in_=z[:, :w], func=ACT.Abs)
             sg = late.tile([P, HALF], BF16, name="sg", bufs=4)
-            nc.scalar.activation(out=sg[:], in_=z[:], func=ACT.Sign)
+            nc.scalar.activation(out=sg[:, :w], in_=z[:, :w], func=ACT.Sign)
             state[i] = az, sg
 
         def add_b(i):
-            dh, g, t = units[i]
+            dh, g, t, c0, w = units[i]
             az, sg = state[i]
-            nc.vector.tensor_tensor(out=az[:], in0=az[:], in1=b_sb[:, HALF * dh : HALF * dh + HALF], op=ALU.add)
+            d0 = HALF * dh + c0
+            nc.vector.tensor_tensor(out=az[:, :w], in0=az[:, :w], in1=b_sb[:, d0 : d0 + w], op=ALU.add)
 
         def signed(i):
-            dh, g, t = units[i]
+            dh, g, t, c0, w = units[i]
             az, sg = state[i]
-            if t == 0:
+            if t == 0 and c0 == 0:
                 o = late.tile([P, 4, HALF], F32, name="o")
                 state["o", dh, g] = o
             o = state["o", dh, g]
-            nc.vector.scalar_tensor_tensor(out=o[:, t, :], in0=az[:], scalar=0.0, in1=sg[:], op0=ALU.max, op1=ALU.mult)
+            nc.vector.scalar_tensor_tensor(out=o[:, t, c0 : c0 + w], in0=az[:, :w], scalar=0.0, in1=sg[:, :w], op0=ALU.max, op1=ALU.mult)
+            d0 = HALF * dh + c0
             nc.sync.dma_start(
-                out=out_0[HALF * g : HALF * g + HALF, HALF * dh : HALF * dh + HALF].rearrange("(c t) e -> c t e", t=4)[:, t, :], in_=o[:, t, :]
+                out=out_0[HALF * g : HALF * g + HALF, d0 : d0 + w].rearrange("(c t) e -> c t e", t=4)[:, t, :], in_=o[:, t, c0 : c0 + w]
             )
 
-        def plane_chunk(dh, g, k):
+        def plane_chunk(dh, g, c0, w, k, eng):
             o = state["o", dh, g]
             if k == 0:
                 il = il_tile()
                 state["il"] = il
             il = state["il"]
-            nc.scalar.copy(
+            (nc.scalar.copy if eng == "s" else nc.vector.tensor_copy)(
                 out=il[:, P * k : P * k + P, :].rearrange("p (c i) t -> p c t i", i=4),
-                in_=o[:, :, P * k : P * k + P].rearrange("p t (c i) -> p c t i", i=4),
+                in_=o[:, :, c0 + P * k : c0 + P * k + P].rearrange("p t (c i) -> p c t i", i=4),
             )
-            if k == 3:
+            if P * k + P == w:
                 oc = late.tile([P, HALF], U32, align_bytes=64, name="oc")
                 os_t = late.tile([P, HALF], U8, align_bytes=64, name="os_t")
-                nc.vector.quantize_mx(out=oc[:].bitcast(FP8X4), scales=os_t[:], in_=il[:].rearrange("p c t -> p (c t)"))
-                d0 = HALF * dh
+                nc.vector.quantize_mx(out=oc[:, :w].bitcast(FP8X4), scales=os_t[:, :w], in_=il[:, :w, :].rearrange("p c t -> p (c t)"))
+                d0 = HALF * dh + c0
                 nc.sync.dma_start(
-                    out=out_1[g, :, d0 : d0 + HALF, :].rearrange("p m t -> p (m t)").bitcast(I32), in_=oc[:].bitcast(I32)
+                    out=out_1[g, :, d0 : d0 + w, :].rearrange("p m t -> p (m t)").bitcast(I32), in_=oc[:, :w].bitcast(I32)
                 )
                 for qd in range(4):
                     nc.sync.dma_start(
-                        out=out_2[g, 4 * qd : 4 * qd + 4, d0 : d0 + HALF].bitcast(I32),
-                        in_=os_t[32 * qd : 32 * qd + 4, :].bitcast(I32),
+                        out=out_2[g, 4 * qd : 4 * qd + 4, d0 : d0 + w].bitcast(I32),
+                        in_=os_t[32 * qd : 32 * qd + 4, :w].bitcast(I32),
                     )
 
         chunks = []
-        for i in range(18):
+        for i in range(len(units) + 2):
             if i >= 2:
                 add_b(i - 2)
-            if i < 16:
+            if i < len(units):
                 add_h(i)
             if chunks:
                 plane_chunk(*chunks.pop(0))
             if i >= 2:
                 signed(i - 2)
-                dh, g, t = units[i - 2]
+                dh, g, t, c0, w = units[i - 2]
                 if t == 3:
-                    chunks += [(dh, g, k) for k in range(4)]
+                    chunks += [(dh, g, c0, w, k, "s") for k in range(w // P)]
         for c in chunks:
-            plane_chunk(*c)
+            plane_chunk(*c[:5], "v" if c[4] == 1 else "s")

@@ -18,12 +18,54 @@ N = 1024
 HALF = 512
 ST_BUFS = 6
 SEQ1 = [
-    ("quad", 0, 0, "svsv"), ("quad", 1, 0, "ssss"), ("sq", 0, 0, "vvv"), ("h", 0, 0), ("h", 0, 1),
-    ("quad", 2, 0, "ssss"), ("sq", 1, 0, "vvv"), ("h", 1, 0), ("h", 1, 1), ("perm", 0, 0),
-    ("quad", 3, 0, "ssss"), ("sq", 2, 0, "vvv"), ("rb", 0, 0), ("kb", 0, 0), ("sq", 3, 0, "vvv"), ("rq", 0, 0), ("kb", 0, 1), ("kq", 0, 0, "s"), ("perm", 1, 0),
-    ("rb", 0, 1), ("kq", 0, 1, "v"), ("rq", 0, 1), ("x", 0, 0), ("x", 0, 1), ("kb", 1, 0), ("kq", 1, 0, "v"), ("x", 1, 0), ("kb", 1, 1), ("x", 1, 1), ("kq", 1, 1, "v"),
-    ("rb", 1, 0), ("rq", 1, 0), ("rb", 1, 1), ("rq", 1, 1),
+    ("quad", 0, 0, "direct"),
+    ("xl", 0, 0),
+    ("quad", 1, 0, ["ssss", "sssv", "ssss", "ssss"]),
+    ("xl", 1, 0),
+    ("h", 0, 0),
+    ("h", 0, 1),
+    ("sq", 1, 0, "v"),
+    ("quad", 2, 0, ["ssss", "ssss", "vsss", "ssss"]),
+    ("h", 1, 0),
+    ("xl", 2, 0),
+    ("sq", 1, 2, "v"),
+    ("sq", 1, 1, "v"),
+    ("sq", 2, 2, "v"),
+    ("sq", 2, 0, "v"),
+    ("quad", 3, 0, ["sssv", "ssss", "ssss", "ssss"]),
+    ("perm", 0, 0),
+    ("h", 1, 1),
+    ("sq", 2, 1, "sv"),
+    ("sq", 3, 0, "v"),
+    ("sq", 3, 1, "v"),
+    ("kb", 0, 0),
+    ("rb", 0, 0),
+    ("kq", 0, 0, "v"),
+    ("perm", 1, 0),
+    ("kb", 0, 1),
+    ("rb", 0, 1),
+    ("xb", 0, 0),
+    ("kb", 1, 0),
+    ("rq", 0, 0),
+    ("xq", 0, 0),
+    ("rq", 0, 1),
+    ("sq", 3, 2, "v"),
+    ("xl", 3, 0),
+    ("kb", 1, 1),
+    ("xb", 0, 1),
+    ("kq", 0, 1, "v"),
+    ("xq", 0, 1),
+    ("kq", 1, 0, "sv"),
+    ("xb", 1, 0),
+    ("rb", 1, 0),
+    ("xb", 1, 1),
+    ("xq", 1, 0),
+    ("kq", 1, 1, "v"),
+    ("xq", 1, 1),
+    ("rb", 1, 1),
+    ("rq", 1, 0),
 ]
+RPOS = {1: [("rq", 1, 1)]}
 FLOPS = 4 * 2 * N * N * N
 
 P0, P1, P2, Q0, Q1, Q2 = range(6)
@@ -33,6 +75,7 @@ NEG_P1, Q2_HALF, Q2_SIXTH = range(3)
 def tile_skewexptaylorrecurrentstep_x2_kernel(tc, h, x, a, t_words, t_scales, p, q, b, out_0, out_1, out_2):
     nc = tc.nc
     with ExitStack() as ctx:
+        ctx.enter_context(tc.manual_schedule())
         keep = ctx.enter_context(tc.tile_pool(name="keep", bufs=1))
         psum = ctx.enter_context(tc.psum_pool(name="psum", bufs=8))
 
@@ -45,7 +88,20 @@ def tile_skewexptaylorrecurrentstep_x2_kernel(tc, h, x, a, t_words, t_scales, p,
             scales = keep.tile([P, 2, N], U8, align_bytes=64, name=nm + "_scales")
             return codes, scales
 
+        pending = []
+
+        def flush():
+            while pending:
+                quantize_now(*pending.pop(0))
+
         def quantize(op, g, c0, il):
+            older = list(pending)
+            pending.clear()
+            pending.append((op, g, c0, il))
+            for args in older:
+                quantize_now(*args)
+
+        def quantize_now(op, g, c0, il):
             codes, scales = op
             nc.vector.quantize_mx(
                 out=codes[:, g, c0 : c0 + HALF].bitcast(FP8X4),
@@ -54,10 +110,13 @@ def tile_skewexptaylorrecurrentstep_x2_kernel(tc, h, x, a, t_words, t_scales, p,
             )
 
         def interleave(il, st, eng="v"):
-            (nc.vector.tensor_copy if eng == "v" else nc.scalar.copy)(
-                out=il[:].rearrange("p (c i) t -> p c t i", i=4),
-                in_=st[:].rearrange("p t (c i) -> p c t i", i=4),
-            )
+            step = HALF // len(eng)
+            for i, e in enumerate(eng):
+                cols = slice(step * i, step * i + step)
+                (nc.vector.tensor_copy if e == "v" else nc.scalar.copy)(
+                    out=il[:, cols, :].rearrange("p (c i) t -> p c t i", i=4),
+                    in_=st[:, :, cols].rearrange("p t (c i) -> p c t i", i=4),
+                )
 
         op_h, op_x, op_k1, op_r = operand("h"), operand("x"), operand("k1"), operand("r")
         op_p1, op_q1, op_q0, op_q0p = operand("p1"), operand("q1"), operand("q0"), operand("q0p")
@@ -121,13 +180,14 @@ def tile_skewexptaylorrecurrentstep_x2_kernel(tc, h, x, a, t_words, t_scales, p,
             for i, (ch, g) in enumerate(quads):
                 an = early.tile([P, 4, HALF], BF16, align_bytes=64, name="raw", bufs=8)
                 ap = early.tile([P, 4, HALF], BF16, align_bytes=64, name="raw", bufs=8)
-                nc.sync.dma_start(
-                    out=an[:],
-                    in_=a[HALF * ch : HALF * ch + HALF, HALF * g : HALF * g + HALF].rearrange("(k c) e -> c k e", c=P),
-                )
+                nat = a[HALF * ch : HALF * ch + HALF, HALF * g : HALF * g + HALF].rearrange("(k c) e -> c k e", c=P)
                 if i == 0:
+                    nc.sync.dma_start(out=an[:, 0:1, :], in_=nat[:, 0:1, :])
                     nc.sync.dma_start(out=pq[0:3, :], in_=p)
                     nc.sync.dma_start(out=pq[3:6, :], in_=q)
+                    nc.sync.dma_start(out=an[:, 1:4, :], in_=nat[:, 1:4, :])
+                else:
+                    nc.sync.dma_start(out=an[:], in_=nat)
                 src = a[HALF * g : HALF * g + HALF, HALF * ch : HALF * ch + HALF].rearrange("(c t) e -> c t e", t=4)
                 for t0, t1 in ((0, 1), (1, 2), (2, 4)) if i == 0 else ((0, 4),):
                     nc.sync.dma_start(out=ap[:, t0:t1, :], in_=src[:, t0:t1, :])
@@ -142,13 +202,14 @@ def tile_skewexptaylorrecurrentstep_x2_kernel(tc, h, x, a, t_words, t_scales, p,
                     in_=t_scales[:, 4 * qd : 4 * qd + 4, :].rearrange("g r n -> r g n").bitcast(I32),
                 )
             nc.sync.dma_start(out=b_sb[:], in_=b.partition_broadcast(P))
-            x_raw = []
-            for i in range(4):
+            x_raw = {}
+
+            def x_load(i):
                 xr = early.tile([P, 2, N], BF16, align_bytes=64, name="raw", bufs=8)
                 nc.sync.dma_start(
                     out=xr[:], in_=x[HALF * (i // 2) : HALF * (i // 2) + HALF, :].rearrange("(c t) e -> c t e", t=4)[:, 2 * (i % 2) : 2 * (i % 2) + 2, :]
                 )
-                x_raw.append(xr)
+                x_raw[i] = xr
 
             gps = psum.tile([P, 8, P], BF16, name="bank")
             for gt in range(8):
@@ -187,12 +248,38 @@ def tile_skewexptaylorrecurrentstep_x2_kernel(tc, h, x, a, t_words, t_scales, p,
                 il = stage.tile([P, HALF, 4], BF16, align_bytes=64, name="il", bufs=4)
                 return il
 
-            def skew_quantize(i, sts, eng="vvv"):
+            def skew_direct(i):
                 ch, g = quads[i]
-                for st, op, e in zip(sts, (op_q0, op_p1, op_q1), eng):
-                    il = il_tile()
-                    interleave(il, st, e)
+                ils = [il_tile() for op in range(3)]
+                for k in range(4):
+                    s = psum.tile([P, 4, P], F32, name="bank")
+                    nc.tensor.matmul(s[:], lhsT=ident[:], rhs=a_perm[ch, g][:, :, P * k : P * k + P], start=True, stop=False)
+                    for t in range(4):
+                        nc.tensor.matmul(s[:, t, :], lhsT=a_nat[ch, g][:, k, t:HALF:4], rhs=nident[:], start=False, stop=(t == 3))
+                    for t in range(4):
+                        gt = 4 * g + t
+                        scaled("s", g_sb[:, gt, HALF * ch + P * k : HALF * ch + P * k + P], s[:, t, :], dv[:, Q2_HALF, gt : gt + 1])
+                    for il, gains in ((ils[0], gn[:, 4 * g : 4 * g + 4, Q0]), (ils[2], gn[:, 4 * g : 4 * g + 4, Q1])):
+                        nc.vector.tensor_tensor(
+                            out=il[:, P * k : P * k + P, :],
+                            in0=s[:].rearrange("p t c -> p c t"),
+                            in1=gains.unsqueeze(1).to_broadcast([P, P, 4]),
+                            op=ALU.mult,
+                        )
+                    nc.vector.tensor_tensor(
+                        out=ils[1][:].rearrange("p (q m) t -> p q m t", q=4)[:, :, 32 * k : 32 * k + 32, :],
+                        in0=s[:].rearrange("p t (m q) -> p q m t", q=4),
+                        in1=dv[:, NEG_P1, 4 * g : 4 * g + 4].unsqueeze(1).unsqueeze(1).to_broadcast([P, 4, 32, 4]),
+                        op=ALU.mult,
+                    )
+                for il, op in zip(ils, (op_q0, op_p1, op_q1)):
                     quantize(op, g, HALF * ch, il)
+
+            def skew_quantize(i, which, st, eng):
+                ch, g = quads[i]
+                il = il_tile()
+                interleave(il, st, eng)
+                quantize((op_q0, op_p1, op_q1)[which], g, HALF * ch, il)
 
             def h_part(n, g):
                 il = il_tile()
@@ -210,7 +297,7 @@ def tile_skewexptaylorrecurrentstep_x2_kernel(tc, h, x, a, t_words, t_scales, p,
                     )
                 quantize(op_h, g, HALF * n, il)
 
-            def x_part(n, g):
+            def x_banks(n, g):
                 il = il_tile()
                 for r in range(2):
                     xt = psum.tile([P, 2, 2, P], F32, name="bank")
@@ -221,18 +308,18 @@ def tile_skewexptaylorrecurrentstep_x2_kernel(tc, h, x, a, t_words, t_scales, p,
                         out=il[:, 256 * r : 256 * r + 256, :].rearrange("p c t -> p (c t)").bitcast(F32).rearrange("p (k r u) -> p k r u", k=2, u=2),
                         in_=xt[:].rearrange("p k u r -> p k r u"),
                     )
-                quantize(op_x, g, HALF * n, il)
+                return il
 
             def permute_q0(j):
-                for g in range(2):
-                    nc.vector.tensor_copy(
-                        out=op_q0p[0][:, g, HALF * j : HALF * j + HALF].bitcast(I32).rearrange("p (q m) -> p q m", q=4),
-                        in_=op_q0[0][:, g, HALF * j : HALF * j + HALF].bitcast(I32).rearrange("p (m q) -> p q m", q=4),
-                    )
-                    nc.vector.tensor_copy(
-                        out=op_q0p[1][:, g, HALF * j : HALF * j + HALF].rearrange("p (q m) -> p q m", q=4),
-                        in_=op_q0[1][:, g, HALF * j : HALF * j + HALF].rearrange("p (m q) -> p q m", q=4),
-                    )
+                cols = slice(HALF * j, HALF * j + HALF)
+                nc.vector.tensor_copy(
+                    out=op_q0p[0][:, :, cols].bitcast(I32).rearrange("p g (q m) -> p g q m", q=4),
+                    in_=op_q0[0][:, :, cols].bitcast(I32).rearrange("p g (m q) -> p g q m", q=4),
+                )
+                nc.vector.tensor_copy(
+                    out=op_q0p[1][:, :, cols].rearrange("p g (q m) -> p g q m", q=4),
+                    in_=op_q0[1][:, :, cols].rearrange("p g (m q) -> p g q m", q=4),
+                )
 
             def k1_banks(j, n):
                 st = stage.tile([P, 4, HALF], BF16, name="st", bufs=ST_BUFS)
@@ -269,21 +356,34 @@ def tile_skewexptaylorrecurrentstep_x2_kernel(tc, h, x, a, t_words, t_scales, p,
             held = {}
             for step in SEQ1:
                 kind, u, v = step[0], step[1], step[2]
-                if kind == "quad":
-                    held["st", u] = skew_quad(*quads[u], who=[step[3]] * 4)
+                if kind == "quad" and step[3] == "direct":
+                    skew_direct(u)
+                elif kind == "quad":
+                    held["st", u] = skew_quad(*quads[u], who=step[3])
                 elif kind == "sq":
-                    skew_quantize(u, held["st", u], step[3])
+                    if ("st", u) in held:
+                        skew_quantize(u, v, held["st", u][v], step[3])
                 elif kind == "h":
                     h_part(u, v)
-                elif kind == "x":
-                    x_part(u, v)
+                elif kind == "xl":
+                    x_load(u)
+                elif kind == "xb":
+                    held["x", u, v] = x_banks(u, v)
+                elif kind == "xq":
+                    quantize(op_x, v, HALF * u, held["x", u, v])
                 elif kind == "perm":
+                    if any(e[0] is op_q0 for e in pending):
+                        flush()
                     permute_q0(u)
                 elif kind == "kb":
+                    if any(e[0] is op_h for e in pending):
+                        flush()
                     held["k", u, v] = k1_banks(u, v)
                 elif kind == "kq":
                     k1_quantize(u, v, held["k", u, v], step[3])
                 elif kind == "rb":
+                    if any(e[0] is op_p1 or e[0] is op_q1 for e in pending):
+                        flush()
                     held["r", u, v] = r_banks(u, v)
                 elif kind == "rq":
                     r_quantize(u, v, held["r", u, v])
@@ -346,6 +446,10 @@ def tile_skewexptaylorrecurrentstep_x2_kernel(tc, h, x, a, t_words, t_scales, p,
                 in_=o[:, :, c0 + P * k : c0 + P * k + P].rearrange("p t (c i) -> p c t i", i=4),
             )
             if P * k + P == w:
+                planes.append((n_step[0] + 1, dh, g, c0, w, il))
+
+        def plane_store(dh, g, c0, w, il):
+            if True:
                 oc = late.tile([P, HALF], U32, align_bytes=64, name="oc")
                 os_t = late.tile([P, HALF], U8, align_bytes=64, name="os_t")
                 nc.vector.quantize_mx(out=oc[:, :w].bitcast(FP8X4), scales=os_t[:, :w], in_=il[:, :w, :].rearrange("p c t -> p (c t)"))
@@ -359,8 +463,17 @@ def tile_skewexptaylorrecurrentstep_x2_kernel(tc, h, x, a, t_words, t_scales, p,
                         in_=os_t[32 * qd : 32 * qd + 4, :w].bitcast(I32),
                     )
 
-        chunks = []
+        chunks, planes, n_step = [], [], [0]
         for i in range(len(units) + 2):
+            n_step[0] = i
+            flush()
+            if planes and planes[0][0] < i:
+                plane_store(*planes.pop(0)[1:])
+            for step in RPOS.get(i, ()):
+                if step[0] == "rb":
+                    held["r", step[1], step[2]] = r_banks(step[1], step[2])
+                else:
+                    r_quantize(step[1], step[2], held["r", step[1], step[2]])
             if i >= 2:
                 add_b(i - 2)
             if i < len(units):
@@ -374,3 +487,5 @@ def tile_skewexptaylorrecurrentstep_x2_kernel(tc, h, x, a, t_words, t_scales, p,
                     chunks += [(dh, g, c0, w, k, "s") for k in range(w // P)]
         for c in chunks:
             plane_chunk(*c[:5], "v" if c[4] == 1 else "s")
+        for pl in planes:
+            plane_store(*pl[1:])

from contextlib import ExitStack

import concourse.mybir as mybir
from concourse.masks import make_identity

F32 = mybir.dt.float32
BF16 = mybir.dt.bfloat16
I32 = mybir.dt.int32
U32 = mybir.dt.uint32
U8 = mybir.dt.uint8
FP8X4 = mybir.dt.float8_e4m3fn_x4
FP4X4 = mybir.dt.float4_e2m1fn_x4
ALU = mybir.AluOpType
ACT = mybir.ActivationFunctionType

P = 128
N = 1024
HALF = 512
ST_BUFS = 6
SEQ1 = [
    ("quad", 0, 0, "direct"),
    ("xl", 0, 0),
    ("quad", 1, 0, ["ssss", "sssv", "ssss", "ssss"]),
    ("xl", 1, 0),
    ("h", 0, 0),
    ("h", 0, 1),
    ("sq", 1, 0, "v"),
    ("quad", 2, 0, ["ssss", "ssss", "vsss", "ssss"]),
    ("h", 1, 0),
    ("xl", 2, 0),
    ("sq", 1, 2, "v"),
    ("sq", 1, 1, "v"),
    ("sq", 2, 2, "v"),
    ("sq", 2, 0, "v"),
    ("quad", 3, 0, ["sssv", "ssss", "ssss", "ssss"]),
    ("perm", 0, 0),
    ("h", 1, 1),
    ("sq", 2, 1, "sv"),
    ("sq", 3, 0, "v"),
    ("sq", 3, 1, "v"),
    ("kb", 0, 0),
    ("rb", 0, 0),
    ("kq", 0, 0, "v"),
    ("perm", 1, 0),
    ("kb", 0, 1),
    ("rb", 0, 1),
    ("xb", 0, 0),
    ("kb", 1, 0),
    ("rq", 0, 0),
    ("xq", 0, 0),
    ("rq", 0, 1),
    ("sq", 3, 2, "v"),
    ("xl", 3, 0),
    ("kb", 1, 1),
    ("xb", 0, 1),
    ("kq", 0, 1, "v"),
    ("xq", 0, 1),
    ("kq", 1, 0, "sv"),
    ("xb", 1, 0),
    ("rb", 1, 0),
    ("xb", 1, 1),
    ("xq", 1, 0),
    ("kq", 1, 1, "v"),
    ("xq", 1, 1),
    ("rb", 1, 1),
    ("rq", 1, 0),
]
RPOS = {1: [("rq", 1, 1)]}
FLOPS = 4 * 2 * N * N * N

P0, P1, P2, Q0, Q1, Q2 = range(6)
NEG_P1, Q2_HALF, Q2_SIXTH = range(3)


def tile_skewexptaylorrecurrentstep_x2_kernel(tc, h, x, a, t_words, t_scales, p, q, b, out_0, out_1, out_2):
    nc = tc.nc
    with ExitStack() as ctx:
        ctx.enter_context(tc.manual_schedule())
        keep = ctx.enter_context(tc.tile_pool(name="keep", bufs=1))
        psum = ctx.enter_context(tc.psum_pool(name="psum", bufs=8))

        def bank():
            bank_t = psum.tile([P, HALF], F32, name="bank")
            return bank_t

        def operand(nm):
            codes = keep.tile([P, 2, N], U32, align_bytes=64, name=nm + "_codes")
            scales = keep.tile([P, 2, N], U8, align_bytes=64, name=nm + "_scales")
            return codes, scales

        pending = []

        def flush():
            while pending:
                quantize_now(*pending.pop(0))

        def quantize(op, g, c0, il):
            older = list(pending)
            pending.clear()
            pending.append((op, g, c0, il))
            for args in older:
                quantize_now(*args)

        def quantize_now(op, g, c0, il):
            codes, scales = op
            nc.vector.quantize_mx(
                out=codes[:, g, c0 : c0 + HALF].bitcast(FP8X4),
                scales=scales[:, g, c0 : c0 + HALF],
                in_=il[:].rearrange("p c t -> p (c t)"),
            )

        def interleave(il, st, eng="v"):
            step = HALF // len(eng)
            for i, e in enumerate(eng):
                cols = slice(step * i, step * i + step)
                (nc.vector.tensor_copy if e == "v" else nc.scalar.copy)(
                    out=il[:, cols, :].rearrange("p (c i) t -> p c t i", i=4),
                    in_=st[:, :, cols].rearrange("p t (c i) -> p c t i", i=4),
                )

        op_h, op_x, op_k1, op_r = operand("h"), operand("x"), operand("k1"), operand("r")
        op_p1, op_q1, op_q0, op_q0p = operand("p1"), operand("q1"), operand("q0"), operand("q0p")
        g_sb = keep.tile([P, 8, N], F32, name="g_sb")
        h_sb = keep.tile([P, 8, N], BF16, align_bytes=64, name="h_sb")
        t_sb = keep.tile([P, 2, 2 * N], U8, align_bytes=64, name="t_sb")
        t_sc = keep.tile([P, 2, N], U8, align_bytes=64, name="t_sc")
        b_sb = keep.tile([P, N], BF16, name="b_sb")
        gn = keep.tile([P, 8, 8], F32, name="gn")
        dv = keep.tile([P, 3, 8], F32, name="dv")
        p0b = keep.tile([P, 8], BF16, name="p0b")
        ident = keep.tile([P, P], BF16, name="ident")
        nident = keep.tile([P, P], BF16, name="nident")
        ident_f = keep.tile([P, P], F32, name="ident_f")

        def scaled(eng, out, in_, sc):
            if eng == "s":
                nc.scalar.activation(out=out, in_=in_, func=ACT.Copy, scale=sc)
            else:
                nc.vector.tensor_scalar(out=out, in0=in_, scalar1=sc, scalar2=None, op0=ALU.mult)

        def product(out, left, m0, right, n0, start=True, stop=True):
            for g in range(2):
                nc.tensor.matmul_mx(
                    out=out,
                    lhsT=left[0][:, g, m0 : m0 + P].bitcast(FP8X4),
                    lhsT_scale=left[1][:, g, m0 : m0 + P],
                    rhs=right[0][:, g, n0 : n0 + HALF].bitcast(FP8X4),
                    rhs_scale=right[1][:, g, n0 : n0 + HALF],
                    start=start and g == 0,
                    stop=stop and g == 1,
                )

        def product_t(out, m0, n0):
            for g in range(2):
                nc.tensor.matmul_mx(
                    out=out,
                    lhsT=op_x[0][:, g, m0 : m0 + P].bitcast(FP8X4),
                    lhsT_scale=op_x[1][:, g, m0 : m0 + P],
                    rhs=t_sb[:, g, 2 * n0 : 2 * n0 + 2 * HALF].bitcast(FP4X4),
                    rhs_scale=t_sc[:, g, n0 : n0 + HALF],
                    start=g == 0,
                    stop=False,
                )

        stage = ctx.enter_context(tc.tile_pool(name="stage", bufs=2))

        with ExitStack() as st1:
            early = st1.enter_context(tc.tile_pool(name="early", bufs=1))

            pq = early.tile([P, N], BF16, name="pq")
            nc.gpsimd.memset(pq[:].bitcast(U32), 0)
            make_identity(nc, ident[:])
            nc.vector.tensor_scalar(out=nident[:], in0=ident[:], scalar1=-1.0, scalar2=None, op0=ALU.mult)
            make_identity(nc, ident_f[:])
            nc.gpsimd.memset(t_sc[:].rearrange("p g n -> p (g n)").bitcast(I32), 0)
            nc.gpsimd.memset(op_q0[1][:].rearrange("p g n -> p (g n)").bitcast(I32), 0)

            quads = [(0, 0), (0, 1), (1, 0), (1, 1)]
            a_nat, a_perm = {}, {}
            for i, (ch, g) in enumerate(quads):
                an = early.tile([P, 4, HALF], BF16, align_bytes=64, name="raw", bufs=8)
                ap = early.tile([P, 4, HALF], BF16, align_bytes=64, name="raw", bufs=8)
                nat = a[HALF * ch : HALF * ch + HALF, HALF * g : HALF * g + HALF].rearrange("(k c) e -> c k e", c=P)
                if i == 0:
                    nc.sync.dma_start(out=an[:, 0:1, :], in_=nat[:, 0:1, :])
                    nc.sync.dma_start(out=pq[0:3, :], in_=p)
                    nc.sync.dma_start(out=pq[3:6, :], in_=q)
                    nc.sync.dma_start(out=an[:, 1:4, :], in_=nat[:, 1:4, :])
                else:
                    nc.sync.dma_start(out=an[:], in_=nat)
                src = a[HALF * g : HALF * g + HALF, HALF * ch : HALF * ch + HALF].rearrange("(c t) e -> c t e", t=4)
                for t0, t1 in ((0, 1), (1, 2), (2, 4)) if i == 0 else ((0, 4),):
                    nc.sync.dma_start(out=ap[:, t0:t1, :], in_=src[:, t0:t1, :])
                a_nat[ch, g], a_perm[ch, g] = an, ap
            for g in range(2):
                nc.sync.dma_start(out=h_sb[:, 4 * g : 4 * g + 4, :], in_=h[HALF * g : HALF * g + HALF, :].rearrange("(c t) e -> c t e", t=4))
            for g in range(2):
                nc.sync.dma_start(out=t_sb[:, g, :].bitcast(I32), in_=t_words[g].bitcast(I32))
            for qd in range(4):
                nc.sync.dma_start(
                    out=t_sc[32 * qd : 32 * qd + 4, :, :].bitcast(I32),
                    in_=t_scales[:, 4 * qd : 4 * qd + 4, :].rearrange("g r n -> r g n").bitcast(I32),
                )
            nc.sync.dma_start(out=b_sb[:], in_=b.partition_broadcast(P))
            x_raw = {}

            def x_load(i):
                xr = early.tile([P, 2, N], BF16, align_bytes=64, name="raw", bufs=8)
                nc.sync.dma_start(
                    out=xr[:], in_=x[HALF * (i // 2) : HALF * (i // 2) + HALF, :].rearrange("(c t) e -> c t e", t=4)[:, 2 * (i % 2) : 2 * (i % 2) + 2, :]
                )
                x_raw[i] = xr

            gps = psum.tile([P, 8, P], BF16, name="bank")
            for gt in range(8):
                g, t = gt // 4, gt % 4
                nc.tensor.transpose(gps[:, gt, :], pq[:, HALF * g + t : HALF * (g + 1) : 4], ident[:])
            nc.vector.tensor_copy(out=gn[:], in_=gps[:, :, 0:8])
            nc.vector.tensor_scalar(out=dv[:, NEG_P1, :], in0=gn[:, :, P1], scalar1=-1.0, scalar2=None, op0=ALU.mult)
            nc.vector.tensor_scalar(out=dv[:, Q2_HALF, :], in0=gn[:, :, Q2], scalar1=0.5, scalar2=None, op0=ALU.mult)
            nc.vector.tensor_scalar(out=dv[:, Q2_SIXTH, :], in0=gn[:, :, Q2], scalar1=1.0 / 6.0, scalar2=None, op0=ALU.mult)
            nc.vector.tensor_copy(out=p0b[:], in_=gn[:, :, P0])

            def skew_quad(ch, g, who):
                sq0 = stage.tile([P, 4, HALF], BF16, name="st", bufs=ST_BUFS)
                sq1 = stage.tile([P, 4, HALF], BF16, name="st", bufs=ST_BUFS)
                sp1 = stage.tile([P, 4, HALF], BF16, name="st", bufs=ST_BUFS)
                for t in range(4):
                    gt = 4 * g + t
                    s = bank()
                    nc.tensor.matmul(s[:], lhsT=ident[:], rhs=a_perm[ch, g][:, t, :], start=True, stop=False)
                    for k in range(4):
                        nc.tensor.matmul(
                            s[:, P * k : P * k + P],
                            lhsT=a_nat[ch, g][:, k, t:HALF:4],
                            rhs=nident[:],
                            start=False,
                            stop=(k == 3),
                        )
                    w = who[t]
                    scaled(w[0], sq0[:, t, :], s[:], gn[:, gt, Q0 : Q0 + 1])
                    scaled(w[1], sp1[:, t, :].rearrange("p (q m) -> p q m", q=4), s[:].rearrange("p (m q) -> p q m", q=4), dv[:, NEG_P1, gt : gt + 1])
                    scaled(w[2], sq1[:, t, :], s[:], gn[:, gt, Q1 : Q1 + 1])
                    scaled(w[3], g_sb[:, gt, HALF * ch : HALF * ch + HALF], s[:], dv[:, Q2_HALF, gt : gt + 1])
                return sq0, sp1, sq1

            def il_tile():
                il = stage.tile([P, HALF, 4], BF16, align_bytes=64, name="il", bufs=4)
                return il

            def skew_direct(i):
                ch, g = quads[i]
                ils = [il_tile() for op in range(3)]
                for k in range(4):
                    s = psum.tile([P, 4, P], F32, name="bank")
                    nc.tensor.matmul(s[:], lhsT=ident[:], rhs=a_perm[ch, g][:, :, P * k : P * k + P], start=True, stop=False)
                    for t in range(4):
                        nc.tensor.matmul(s[:, t, :], lhsT=a_nat[ch, g][:, k, t:HALF:4], rhs=nident[:], start=False, stop=(t == 3))
                    for t in range(4):
                        gt = 4 * g + t
                        scaled("s", g_sb[:, gt, HALF * ch + P * k : HALF * ch + P * k + P], s[:, t, :], dv[:, Q2_HALF, gt : gt + 1])
                    for il, gains in ((ils[0], gn[:, 4 * g : 4 * g + 4, Q0]), (ils[2], gn[:, 4 * g : 4 * g + 4, Q1])):
                        nc.vector.tensor_tensor(
                            out=il[:, P * k : P * k + P, :],
                            in0=s[:].rearrange("p t c -> p c t"),
                            in1=gains.unsqueeze(1).to_broadcast([P, P, 4]),
                            op=ALU.mult,
                        )
                    nc.vector.tensor_tensor(
                        out=ils[1][:].rearrange("p (q m) t -> p q m t", q=4)[:, :, 32 * k : 32 * k + 32, :],
                        in0=s[:].rearrange("p t (m q) -> p q m t", q=4),
                        in1=dv[:, NEG_P1, 4 * g : 4 * g + 4].unsqueeze(1).unsqueeze(1).to_broadcast([P, 4, 32, 4]),
                        op=ALU.mult,
                    )
                for il, op in zip(ils, (op_q0, op_p1, op_q1)):
                    quantize(op, g, HALF * ch, il)

            def skew_quantize(i, which, st, eng):
                ch, g = quads[i]
                il = il_tile()
                interleave(il, st, eng)
                quantize((op_q0, op_p1, op_q1)[which], g, HALF * ch, il)

            def h_part(n, g):
                il = il_tile()
                words = h_sb[:].bitcast(F32)
                for r in range(2):
                    ht = psum.tile([P, 2, P, 2], F32, name="bank")
                    for k in range(2):
                        for u in range(2):
                            nc.tensor.transpose(ht[:, k, :, u], words[:, 4 * n + 2 * r + k, 256 * g + u : 256 * (g + 1) : 2], ident_f[:])
                    nc.vector.tensor_tensor(
                        out=il[:, 256 * r : 256 * r + 256, :],
                        in0=ht[:].rearrange("p k r u -> p (k r u)").bitcast(BF16).rearrange("p (c t) -> p c t", t=4),
                        in1=p0b[:, 4 * g : 4 * g + 4].unsqueeze(1).to_broadcast([P, 256, 4]),
                        op=ALU.mult,
                    )
                quantize(op_h, g, HALF * n, il)

            def x_banks(n, g):
                il = il_tile()
                for r in range(2):
                    xt = psum.tile([P, 2, 2, P], F32, name="bank")
                    for k in range(2):
                        for u in range(2):
                            nc.tensor.transpose(xt[:, k, u, :], x_raw[2 * n + r][:].bitcast(F32)[:, k, 256 * g + u : 256 * (g + 1) : 2], ident_f[:])
                    nc.scalar.copy(
                        out=il[:, 256 * r : 256 * r + 256, :].rearrange("p c t -> p (c t)").bitcast(F32).rearrange("p (k r u) -> p k r u", k=2, u=2),
                        in_=xt[:].rearrange("p k u r -> p k r u"),
                    )
                return il

            def permute_q0(j):
                cols = slice(HALF * j, HALF * j + HALF)
                nc.vector.tensor_copy(
                    out=op_q0p[0][:, :, cols].bitcast(I32).rearrange("p g (q m) -> p g q m", q=4),
                    in_=op_q0[0][:, :, cols].bitcast(I32).rearrange("p g (m q) -> p g q m", q=4),
                )
                nc.vector.tensor_copy(
                    out=op_q0p[1][:, :, cols].rearrange("p g (q m) -> p g q m", q=4),
                    in_=op_q0[1][:, :, cols].rearrange("p g (m q) -> p g q m", q=4),
                )

            def k1_banks(j, n):
                st = stage.tile([P, 4, HALF], BF16, name="st", bufs=ST_BUFS)
                for t in range(4):
                    kb = bank()
                    product(kb[:], op_q0p, HALF * j + P * t, op_h, HALF * n)
                    scaled("s", st[:, t, :], kb[:], gn[:, 4 * j + t, P2 : P2 + 1])
                return st

            def k1_quantize(j, n, st, eng="v"):
                il = il_tile()
                interleave(il, st, eng)
                quantize(op_k1, j, HALF * n, il)


            def r_banks(dh, j):
                tt = stage.tile([P, 4, HALF], F32, name="tt")
                for t in range(4):
                    sb = bank()
                    product(sb[:], op_p1, HALF * j + P * t, op_q1, HALF * dh)
                    scaled("s", tt[:, t, :], sb[:], dv[:, Q2_SIXTH, 4 * j + t : 4 * j + t + 1])
                return tt

            def r_quantize(dh, j, tt):
                il = il_tile()
                nc.vector.tensor_tensor(
                    out=il[:].rearrange("p (c i) t -> p c t i", i=4),
                    in0=tt[:].rearrange("p t (c i) -> p c t i", i=4),
                    in1=g_sb[:, 4 * j : 4 * j + 4, HALF * dh : HALF * dh + HALF].rearrange("p t (c i) -> p c t i", i=4),
                    op=ALU.add,
                )
                quantize(op_r, j, HALF * dh, il)

            held = {}
            for step in SEQ1:
                kind, u, v = step[0], step[1], step[2]
                if kind == "quad" and step[3] == "direct":
                    skew_direct(u)
                elif kind == "quad":
                    held["st", u] = skew_quad(*quads[u], who=step[3])
                elif kind == "sq":
                    if ("st", u) in held:
                        skew_quantize(u, v, held["st", u][v], step[3])
                elif kind == "h":
                    h_part(u, v)
                elif kind == "xl":
                    x_load(u)
                elif kind == "xb":
                    held["x", u, v] = x_banks(u, v)
                elif kind == "xq":
                    quantize(op_x, v, HALF * u, held["x", u, v])
                elif kind == "perm":
                    if any(e[0] is op_q0 for e in pending):
                        flush()
                    permute_q0(u)
                elif kind == "kb":
                    if any(e[0] is op_h for e in pending):
                        flush()
                    held["k", u, v] = k1_banks(u, v)
                elif kind == "kq":
                    k1_quantize(u, v, held["k", u, v], step[3])
                elif kind == "rb":
                    if any(e[0] is op_p1 or e[0] is op_q1 for e in pending):
                        flush()
                    held["r", u, v] = r_banks(u, v)
                elif kind == "rq":
                    r_quantize(u, v, held["r", u, v])

        late = ctx.enter_context(tc.tile_pool(name="late", bufs=2))
        QUART = HALF // 2
        units = [(dh, g, t, 0, HALF) for dh in range(2) for g in range(2) for t in range(4)]
        units = units[:12] + [(1, 1, t, QUART * c, QUART) for c in range(2) for t in range(4)]
        state = {}

        def z_bank(dh, g, t):
            zb = bank()
            m0, d0 = HALF * g + P * t, HALF * dh
            product_t(zb[:], m0, d0)
            product(zb[:], op_h, m0, op_q0, d0, start=False, stop=False)
            product(zb[:], op_k1, m0, op_r, d0, start=False, stop=True)
            return zb

        def add_h(i):
            dh, g, t, c0, w = units[i]
            if c0 == 0:
                state["z", dh, g, t] = z_bank(dh, g, t)
            zb = state["z", dh, g, t]
            d0 = HALF * dh + c0
            z = late.tile([P, HALF], F32, name="z", bufs=3)
            nc.vector.tensor_tensor(out=z[:, :w], in0=zb[:, c0 : c0 + w], in1=h_sb[:, 4 * g + t, d0 : d0 + w], op=ALU.add)
            az = late.tile([P, HALF], F32, name="az", bufs=4)
            nc.scalar.activation(out=az[:, :w], in_=z[:, :w], func=ACT.Abs)
            sg = late.tile([P, HALF], BF16, name="sg", bufs=4)
            nc.scalar.activation(out=sg[:, :w], in_=z[:, :w], func=ACT.Sign)
            state[i] = az, sg

        def add_b(i):
            dh, g, t, c0, w = units[i]
            az, sg = state[i]
            d0 = HALF * dh + c0
            nc.vector.tensor_tensor(out=az[:, :w], in0=az[:, :w], in1=b_sb[:, d0 : d0 + w], op=ALU.add)

        def signed(i):
            dh, g, t, c0, w = units[i]
            az, sg = state[i]
            if t == 0 and c0 == 0:
                o = late.tile([P, 4, HALF], F32, name="o")
                state["o", dh, g] = o
            o = state["o", dh, g]
            nc.vector.scalar_tensor_tensor(out=o[:, t, c0 : c0 + w], in0=az[:, :w], scalar=0.0, in1=sg[:, :w], op0=ALU.max, op1=ALU.mult)
            d0 = HALF * dh + c0
            nc.sync.dma_start(
                out=out_0[HALF * g : HALF * g + HALF, d0 : d0 + w].rearrange("(c t) e -> c t e", t=4)[:, t, :], in_=o[:, t, c0 : c0 + w]
            )

        def plane_chunk(dh, g, c0, w, k, eng):
            o = state["o", dh, g]
            if k == 0:
                il = il_tile()
                state["il"] = il
            il = state["il"]
            (nc.scalar.copy if eng == "s" else nc.vector.tensor_copy)(
                out=il[:, P * k : P * k + P, :].rearrange("p (c i) t -> p c t i", i=4),
                in_=o[:, :, c0 + P * k : c0 + P * k + P].rearrange("p t (c i) -> p c t i", i=4),
            )
            if P * k + P == w:
                planes.append((n_step[0] + 1, dh, g, c0, w, il))

        def plane_store(dh, g, c0, w, il):
            if True:
                oc = late.tile([P, HALF], U32, align_bytes=64, name="oc")
                os_t = late.tile([P, HALF], U8, align_bytes=64, name="os_t")
                nc.vector.quantize_mx(out=oc[:, :w].bitcast(FP8X4), scales=os_t[:, :w], in_=il[:, :w, :].rearrange("p c t -> p (c t)"))
                d0 = HALF * dh + c0
                nc.sync.dma_start(
                    out=out_1[g, :, d0 : d0 + w, :].rearrange("p m t -> p (m t)").bitcast(I32), in_=oc[:, :w].bitcast(I32)
                )
                for qd in range(4):
                    nc.sync.dma_start(
                        out=out_2[g, 4 * qd : 4 * qd + 4, d0 : d0 + w].bitcast(I32),
                        in_=os_t[32 * qd : 32 * qd + 4, :w].bitcast(I32),
                    )

        chunks, planes, n_step = [], [], [0]
        for i in range(len(units) + 2):
            n_step[0] = i
            flush()
            if planes and planes[0][0] < i:
                plane_store(*planes.pop(0)[1:])
            for step in RPOS.get(i, ()):
                if step[0] == "rb":
                    held["r", step[1], step[2]] = r_banks(step[1], step[2])
                else:
                    r_quantize(step[1], step[2], held["r", step[1], step[2]])
            if i >= 2:
                add_b(i - 2)
            if i < len(units):
                add_h(i)
            if chunks:
                plane_chunk(*chunks.pop(0))
            if i >= 2:
                signed(i - 2)
                dh, g, t, c0, w = units[i - 2]
                if t == 3:
                    chunks += [(dh, g, c0, w, k, "s") for k in range(w // P)]
        for c in chunks:
            plane_chunk(*c[:5], "v" if c[4] == 1 else "s")
        for pl in planes:
            plane_store(*pl[1:])
